import numpy as np
import ml_dtypes


def mxq(x, axis, fmt="e4m3"):
    dtype, down = {"e4m3": (ml_dtypes.float8_e4m3fn, 7), "e5m2": (ml_dtypes.float8_e5m2, 14)}[fmt]
    v = np.moveaxis(np.asarray(x, np.float32).astype(ml_dtypes.bfloat16).astype(np.float64), axis, -1)
    blocks = v.reshape(v.shape[:-1] + (-1, 32))
    amax = np.abs(blocks).max(-1, keepdims=True)
    byte = np.maximum(np.where(amax > 0, np.frexp(amax)[1] - 1 + 127, 0) - down, 1)
    scale = np.exp2(byte - 127.0)
    codes = (blocks / scale).astype(np.float32).astype(dtype).astype(np.float64)
    return np.moveaxis((codes * scale).reshape(v.shape), -1, axis)


WIDE = False


def mx_kscale(k):
    if not WIDE:
        return np.ones(k)
    levels = np.array([10, -10, 5, -5, 0])
    if k % 512:
        return np.exp2(np.random.permutation(np.resize(levels, k // 32))).repeat(32)
    a = np.empty((k // 512, 16))
    for p in range(k // 512):
        a[p, :8] = np.random.permutation(np.resize(levels, 8))
        for g in range(8):
            far = levels[np.abs(levels - a[p, g]) >= 10]
            a[p, g + 8] = far[np.random.randint(len(far))]
    return np.exp2(a.ravel()).repeat(32)


def f64(x):
    return np.asarray(x).astype(np.float64)


def striped8(idx):
    return np.concatenate([x.reshape(-1, 16).T for x in idx]).astype(np.uint16)


def runs(offs, k):
    lists = np.stack([offs[16 * r : 16 * r + 16].T.reshape(-1) for r in range(8)]).astype(np.int64)
    return lists[np.arange(k) % 512 // 64]


def pack_weight(w):
    k, n = w.shape
    w = f64(np.asarray(w, np.float32).astype(ml_dtypes.bfloat16)).reshape(k // 32, 32, n)
    amax = np.abs(w).max(1)
    byte = np.clip(np.where(amax > 0, np.frexp(amax)[1] - 1 + 127 - 7, 1), 1, 254)
    scaled = (w * np.exp2(127.0 - byte)[:, None, :]).reshape(k, n).astype(np.float32)
    words = np.ascontiguousarray(scaled.reshape(k // 512, 128, 4, n).transpose(0, 1, 3, 2)).astype(ml_dtypes.float8_e4m3fn).view(np.uint8)
    return words, np.ascontiguousarray(byte.astype(np.uint8).reshape(k // 512, 16, n))


def unpack_weight(words, scales):
    g, p, n, _ = words.shape
    vals = np.ascontiguousarray(words).view(ml_dtypes.float8_e4m3fn).astype(np.float64) * np.repeat(np.exp2(scales.astype(np.float64) - 127.0), 8, axis=1)[..., None]
    return vals.transpose(0, 1, 3, 2).reshape(g * 512, n)


K, T, S, N, H = 512, 2048, 512, 512, 512


def setup_inputs():
    n = np.random.standard_normal
    s = mx_kscale(K)[:, None]
    u = mx_kscale(H)
    packed_xT = pack_weight(n((K, T)) * s)
    return {
        "x_words": packed_xT[0],
        "x_scales": packed_xT[1],
        "w1": (n((K, H)) / np.sqrt(K) / s).astype(np.float32),
        "gn": (np.random.uniform(0.5, 1.5, (H, 1)) * u[:, None]).astype(np.float32),
        "w2": (n((H, N)) / np.sqrt(H) / u[:, None]).astype(np.float32),
        "offs": striped8(np.random.randint(0, T, (8, S))),
        "n1": striped8(np.stack([np.random.permutation(S) for _ in range(8)])),
        "n2": striped8(np.stack([np.random.permutation(S) for _ in range(8)])),
        "n3": striped8(np.stack([np.random.permutation(S) for _ in range(8)])),
    }


def reference(x_words, x_scales, w1, gn, w2, offs, n1, n2, n3):
    xq = unpack_weight(x_words, x_scales)[np.arange(K)[:, None], runs(offs, K)]
    y = mxq(f64(w1), 0, "e4m3").T @ xq
    st = y - (y[np.arange(H)[:, None], runs(n1, H)])
    z = f64(gn) * (st - (0.5 * (st[np.arange(H)[:, None], runs(n1, H)])))
    h = mxq(f64(w2), 0, "e4m3").T @ mxq(z, 0, "e4m3")
    pa = h[np.arange(N)[:, None], runs(n2, N)]
    pb = h[np.arange(N)[:, None], runs(n3, N)]
    return np.maximum(np.minimum(h, pa), np.minimum(np.maximum(h, pa), pb))

@@ -1,0 +1,175 @@
+from contextlib import ExitStack
+
+import concourse.mybir as mybir
+
+F32 = mybir.dt.float32
+BF16 = mybir.dt.bfloat16
+I32 = mybir.dt.int32
+U32 = mybir.dt.uint32
+U16 = mybir.dt.uint16
+U8 = mybir.dt.uint8
+FP8X4 = mybir.dt.float8_e4m3fn_x4
+ALU = mybir.AluOpType
+COPY = mybir.ActivationFunctionType.Copy
+
+P = 128
+T, S = 2048, 512
+HALF = S // 2
+LIST_COLS = S // 16
+FLOPS = 2 * 2 * 512 * 512 * 512
+
+
+def tile_picked_hashtwicemed_none_p_kernel(
+    tc, x_words, x_scales, w1, gn, w2, offs, n1, n2, n3, out
+):
+    nc = tc.nc
+    with ExitStack() as ctx:
+        lists = ctx.enter_context(tc.tile_pool(name="lists", bufs=1))
+        sb = ctx.enter_context(tc.tile_pool(name="sb", bufs=1))
+        psum = ctx.enter_context(tc.psum_pool(name="psum", bufs=1))
+
+        offs_t = lists.tile([P, LIST_COLS], U16, name="offs_t")
+        n1_t = lists.tile([P, LIST_COLS], U16, name="n1_t")
+        n2_t = lists.tile([P, LIST_COLS], U16, name="n2_t")
+        n3_t = lists.tile([P, LIST_COLS], U16, name="n3_t")
+
+        scale_table = sb.tile([P, T], U8, name="scale_table", tag="x_shared", align_bytes=64)
+        x_plane = sb.tile([P, S], U8, name="x_plane", align_bytes=64)
+        word_table = sb.tile([P, T], I32, name="word_table", align_bytes=64)
+        w1_raw = sb.tile([P, 4, 512], F32, name="w1_raw", tag="w_raw")
+        gain = sb.tile([P, 4], F32, name="gain")
+
+        nc.vector.memset(scale_table[:].bitcast(I32), 0)
+        nc.vector.memset(x_plane[:].bitcast(I32), 0)
+        nc.scalar.dma_start(word_table[:], x_words[0].rearrange("p c r -> p (c r)").bitcast(I32))
+        nc.sync.dma_start(offs_t[:], offs)
+        nc.sync.dma_start(n1_t[:], n1)
+        nc.sync.dma_start(n2_t[:], n2)
+        nc.sync.dma_start(n3_t[:], n3)
+        nc.sync.dma_start(gain[:], gn.rearrange("(p t) o -> p (t o)", t=4))
+        nc.sync.dma_start(scale_table[0:P:8, :].bitcast(I32), x_scales[0].bitcast(I32))
+        nc.sync.dma_start(w1_raw[:], w1.rearrange("(p j) c -> p j c", j=4))
+
+        windows = [sb.tile([P, 2 * S], F32, name=f"window{t}") for t in range(4)]
+        for t in range(4):
+            nc.vector.memset(windows[t][:, S:], 0.0)
+
+        picked_scales = sb.tile([P, S], U8, name="picked_scales", align_bytes=64)
+        nc.vector.tensor_copy(picked_scales[:], scale_table[:].indirect(offs_t[:]))
+        for s in range(4):
+            nc.sync.dma_start(x_plane[s:P:32, :].bitcast(I32), picked_scales[8 * s : P : 32, :].bitcast(I32))
+        x_codes = sb.tile([P, S], U32, name="x_codes", tag="x_shared", align_bytes=64)
+        nc.vector.tensor_copy(x_codes[:], word_table[:].bitcast(U32).indirect(offs_t[:]))
+
+        w1_codes = [sb.tile([P, P], U32, name=f"w1_codes{t}", align_bytes=64) for t in range(4)]
+        w1_planes = [sb.tile([P, P], U8, name=f"w1_plane{t}", align_bytes=64) for t in range(4)]
+        w1_bf = [sb.tile([P, 2, P, 4], BF16, name=f"w1_bf{u}", align_bytes=64) for u in range(2)]
+        w1_view = w1_raw[:].rearrange("p j (m t) -> p m t j", t=4)
+        nc.vector.tensor_copy(w1_bf[0][:].rearrange("p t m j -> p m t j"), w1_view[:, :, 0:2, :])
+        nc.scalar.copy(w1_bf[1][:].rearrange("p t m j -> p m t j"), w1_view[:, :, 2:4, :])
+
+        y_ps = [psum.tile([P, S], F32, name=f"y_ps{t}") for t in range(4)]
+        h_ps = [psum.tile([P, S], F32, name=f"h_ps{t}") for t in range(4)]
+        plain = [sb.tile([P, S], F32, name=f"plain{t}") for t in range(4)]
+        for t in range(4):
+            nc.vector.quantize_mx(
+                out=w1_codes[t][:].bitcast(FP8X4),
+                scales=w1_planes[t][:],
+                in_=w1_bf[t // 2][:, t % 2].rearrange("p m j -> p (m j)"),
+            )
+            nc.tensor.matmul_mx(
+                out=y_ps[t][:], lhsT=w1_codes[t][:].bitcast(FP8X4), lhsT_scale=w1_planes[t][:],
+                rhs=x_codes[:].bitcast(FP8X4), rhs_scale=x_plane[:], start=True, stop=True,
+            )
+            nc.scalar.activation(windows[t][:, :S], y_ps[t][:], COPY, scale=gain[:, t : t + 1])
+            nc.scalar.activation(plain[t][:], y_ps[t][:], COPY, scale=gain[:, t : t + 1])
+
+        w2_raw = sb.tile([P, 4, 512], F32, name="w2_raw", tag="w_raw")
+        nc.sync.dma_start(w2_raw[:], w2.rearrange("(p j) c -> p j c", j=4))
+
+        neg_st = [sb.tile([P, S], F32, name=f"neg_st{t}") for t in range(4)]
+        twice = [sb.tile([P, S], F32, name=f"twice{t}") for t in range(4)]
+        for t in range(4):
+            nc.vector.tensor_tensor(neg_st[t][:], windows[t][:].indirect(n1_t[:]), plain[t][:], ALU.subtract)
+            nc.scalar.activation(twice[t][:], neg_st[t][:], COPY, scale=2.0)
+
+        z_bf = []
+        for u in range(2):
+            cols = slice(u * HALF, (u + 1) * HALF)
+            z4 = sb.tile([P, 4, HALF], F32, name=f"z4_{u}")
+            for t in range(4):
+                nc.vector.tensor_tensor(
+                    z4[:, t, :], neg_st[t][:].indirect(n1_t[:, u * 16 : (u + 1) * 16]), twice[t][:, cols], ALU.subtract
+                )
+            zb = sb.tile([P, HALF, 4], BF16, name=f"z_bf{u}", align_bytes=64)
+            nc.scalar.activation(
+                zb[:].rearrange("p (c i) t -> p c t i", i=4), z4[:].rearrange("p t (c i) -> p c t i", i=4), COPY, scale=0.5
+            )
+            z_bf.append(zb)
+
+        w2_codes = [sb.tile([P, P], U32, name=f"w2_codes{t}", align_bytes=64) for t in range(4)]
+        w2_planes = [sb.tile([P, P], U8, name=f"w2_plane{t}", align_bytes=64) for t in range(4)]
+        w2_bf = [sb.tile([P, P, 4], BF16, name=f"w2_bf{t}", align_bytes=64) for t in range(4)]
+        w2_view = w2_raw[:].rearrange("p j (b t r) -> p t b r j", t=4, r=8)
+        z_codes = [sb.tile([P, HALF], U32, name=f"z_codes{u}", align_bytes=64) for u in range(2)]
+        z_planes = [sb.tile([P, HALF], U8, name=f"z_plane{u}", align_bytes=64) for u in range(2)]
+
+        def quantize_z(u):
+            nc.vector.quantize_mx(
+                out=z_codes[u][:].bitcast(FP8X4), scales=z_planes[u][:], in_=z_bf[u][:].rearrange("p c t -> p (c t)")
+            )
+
+        def quantize_w2(t):
+            nc.vector.quantize_mx(
+                out=w2_codes[t][:].bitcast(FP8X4), scales=w2_planes[t][:], in_=w2_bf[t][:].rearrange("p m j -> p (m j)")
+            )
+
+        def cast_w2(t):
+            nc.vector.tensor_copy(w2_bf[t][:].rearrange("p (b r) j -> p b r j", r=8), w2_view[:, t])
+
+        quantize_z(0)
+        cast_w2(0)
+        cast_w2(1)
+        quantize_w2(0)
+        quantize_z(1)
+        quantize_w2(1)
+        cast_w2(2)
+        cast_w2(3)
+        quantize_w2(2)
+        quantize_w2(3)
+
+        for t in range(4):
+            for u in range(2):
+                nc.tensor.matmul_mx(
+                    out=h_ps[t][:, u * HALF : (u + 1) * HALF], lhsT=w2_codes[t][:].bitcast(FP8X4), lhsT_scale=w2_planes[t][:],
+                    rhs=z_codes[u][:].bitcast(FP8X4), rhs_scale=z_planes[u][:], start=True, stop=True,
+                )
+            nc.scalar.copy(windows[t][:, :S], h_ps[t][:])
+            nc.scalar.copy(plain[t][:], h_ps[t][:])
+
+        out_view = out.rearrange("(b t r) n -> t b r n", t=4, r=8)
+        pieces = [(0, 0, S), (1, 0, S), (2, 0, S), (3, 0, HALF), (3, HALF, S)]
+        held = {}
+
+        def fetch(i):
+            t, a, b = pieces[i]
+            d1 = sb.tile([P, b - a], F32, name=f"d1_{i}")
+            d2 = sb.tile([P, b - a], F32, name=f"d2_{i}")
+            nc.vector.tensor_tensor(d1[:], windows[t][:].indirect(n2_t[:, a // 16 : b // 16]), plain[t][:, a:b], ALU.subtract)
+            nc.vector.tensor_tensor(d2[:], windows[t][:].indirect(n3_t[:, a // 16 : b // 16]), plain[t][:, a:b], ALU.subtract)
+            held[i] = (d1, d2)
+
+        def finish(i):
+            t, a, b = pieces[i]
+            d1, d2 = held[i]
+            upper = sb.tile([P, b - a], F32, name=f"upper{i}")
+            mid = sb.tile([P, b - a], F32, name=f"mid{i}")
+            res = sb.tile([P, b - a], F32, name=f"res{i}")
+            nc.vector.scalar_tensor_tensor(upper[:], d1[:], 0.0, d2[:], ALU.max, ALU.min)
+            nc.vector.scalar_tensor_tensor(mid[:], d1[:], 0.0, upper[:], ALU.min, ALU.max)
+            nc.vector.tensor_tensor(res[:], mid[:], plain[t][:, a:b], ALU.add)
+            nc.sync.dma_start(out_view[t][:, :, a:b], res[:])
+
+        for i in range(len(pieces)):
+            fetch(i)
+            finish(i)

@@ -1,6 +1,7 @@
 from contextlib import ExitStack
 
 import concourse.mybir as mybir
+from concourse.masks import make_identity
 
 F32 = mybir.dt.float32
 BF16 = mybir.dt.bfloat16
@@ -17,6 +18,7 @@ T, S = 2048, 512
 HALF = S // 2
 LIST_COLS = S // 16
 FLOPS = 2 * 2 * 512 * 512 * 512
+Z_SLICES = ((0, 256), (256, 384), (384, 512))
 
 
 def tile_picked_hashtwicemed_none_p_kernel(
@@ -33,143 +35,211 @@ def tile_picked_hashtwicemed_none_p_kernel(
         n2_t = lists.tile([P, LIST_COLS], U16, name="n2_t")
         n3_t = lists.tile([P, LIST_COLS], U16, name="n3_t")
 
-        scale_table = sb.tile([P, T], U8, name="scale_table", tag="x_shared", align_bytes=64)
-        x_plane = sb.tile([P, S], U8, name="x_plane", align_bytes=64)
-        word_table = sb.tile([P, T], I32, name="word_table", align_bytes=64)
-        w1_raw = sb.tile([P, 4, 512], F32, name="w1_raw", tag="w_raw")
-        gain = sb.tile([P, 4], F32, name="gain")
+        def entries(list_tile, a, b):
+            return list_tile[:, a // 16 : b // 16]
 
-        nc.vector.memset(scale_table[:].bitcast(I32), 0)
+        scale_table = sb.tile([P, T], U8, name="scale_table", tag="after_scales", align_bytes=64)
+        x_plane = sb.tile([P, S], U8, name="x_plane", align_bytes=64)
+        word_table = sb.tile([P, T], I32, name="word_table", tag="after_words", align_bytes=64)
+        w1_raw = sb.tile([P, 4, 512], F32, name="w1_raw")
+        gain = sb.tile([P, 4], F32, name="gain")
+        ident = sb.tile([P, P], F32, name="ident")
+
+        scale_words = scale_table[:].bitcast(I32)
+        nc.vector.memset(scale_words[:, : T // 8], 0)
+        nc.gpsimd.memset(scale_words[:, T // 8 :], 0)
         nc.vector.memset(x_plane[:].bitcast(I32), 0)
-        nc.scalar.dma_start(word_table[:], x_words[0].rearrange("p c r -> p (c r)").bitcast(I32))
         nc.sync.dma_start(offs_t[:], offs)
-        nc.sync.dma_start(n1_t[:], n1)
-        nc.sync.dma_start(n2_t[:], n2)
-        nc.sync.dma_start(n3_t[:], n3)
         nc.sync.dma_start(gain[:], gn.rearrange("(p t) o -> p (t o)", t=4))
         nc.sync.dma_start(scale_table[0:P:8, :].bitcast(I32), x_scales[0].bitcast(I32))
         nc.sync.dma_start(w1_raw[:], w1.rearrange("(p j) c -> p j c", j=4))
+        nc.sync.dma_start(word_table[:], x_words[0].rearrange("p c r -> p (c r)").bitcast(I32))
+        nc.sync.dma_start(n1_t[:], n1)
+        nc.sync.dma_start(n2_t[:], n2)
+        nc.sync.dma_start(n3_t[:], n3)
 
         windows = [sb.tile([P, 2 * S], F32, name=f"window{t}") for t in range(4)]
-        for t in range(4):
+        for t in range(0, 4, 2):
             nc.vector.memset(windows[t][:, S:], 0.0)
+            nc.scalar.copy(windows[t + 1][:, S:], windows[t][:, S:])
+        make_identity(nc, ident[:])
 
         picked_scales = sb.tile([P, S], U8, name="picked_scales", align_bytes=64)
         nc.vector.tensor_copy(picked_scales[:], scale_table[:].indirect(offs_t[:]))
         for s in range(4):
-            nc.sync.dma_start(x_plane[s:P:32, :].bitcast(I32), picked_scales[8 * s : P : 32, :].bitcast(I32))
-        x_codes = sb.tile([P, S], U32, name="x_codes", tag="x_shared", align_bytes=64)
-        nc.vector.tensor_copy(x_codes[:], word_table[:].bitcast(U32).indirect(offs_t[:]))
+            nc.scalar.dma_start(x_plane[s:P:32, :].bitcast(I32), picked_scales[8 * s : P : 32, :].bitcast(I32))
 
         w1_codes = [sb.tile([P, P], U32, name=f"w1_codes{t}", align_bytes=64) for t in range(4)]
         w1_planes = [sb.tile([P, P], U8, name=f"w1_plane{t}", align_bytes=64) for t in range(4)]
-        w1_bf = [sb.tile([P, 2, P, 4], BF16, name=f"w1_bf{u}", align_bytes=64) for u in range(2)]
+        w1_lo = sb.tile([P, 2, P, 4], BF16, name="w1_lo", tag="after_scales", align_bytes=64)
+        w1_hi = sb.tile([P, 2, P, 4], BF16, name="w1_hi", align_bytes=64)
+        w1_bf = [w1_lo, w1_hi]
         w1_view = w1_raw[:].rearrange("p j (m t) -> p m t j", t=4)
-        nc.vector.tensor_copy(w1_bf[0][:].rearrange("p t m j -> p m t j"), w1_view[:, :, 0:2, :])
-        nc.scalar.copy(w1_bf[1][:].rearrange("p t m j -> p m t j"), w1_view[:, :, 2:4, :])
-
-        y_ps = [psum.tile([P, S], F32, name=f"y_ps{t}") for t in range(4)]
-        h_ps = [psum.tile([P, S], F32, name=f"h_ps{t}") for t in range(4)]
-        plain = [sb.tile([P, S], F32, name=f"plain{t}") for t in range(4)]
+        nc.vector.tensor_copy(w1_lo[:].rearrange("p t m j -> p m t j"), w1_view[:, :, 0:2, :])
+        nc.scalar.copy(w1_hi[:].rearrange("p t m j -> p m t j"), w1_view[:, :, 2:4, :])
         for t in range(4):
             nc.vector.quantize_mx(
                 out=w1_codes[t][:].bitcast(FP8X4),
                 scales=w1_planes[t][:],
                 in_=w1_bf[t // 2][:, t % 2].rearrange("p m j -> p (m j)"),
             )
-            nc.tensor.matmul_mx(
-                out=y_ps[t][:], lhsT=w1_codes[t][:].bitcast(FP8X4), lhsT_scale=w1_planes[t][:],
-                rhs=x_codes[:].bitcast(FP8X4), rhs_scale=x_plane[:], start=True, stop=True,
-            )
-            nc.scalar.activation(windows[t][:, :S], y_ps[t][:], COPY, scale=gain[:, t : t + 1])
-            nc.scalar.activation(plain[t][:], y_ps[t][:], COPY, scale=gain[:, t : t + 1])
 
-        w2_raw = sb.tile([P, 4, 512], F32, name="w2_raw", tag="w_raw")
+        x_codes = sb.tile([P, S], U32, name="x_codes", align_bytes=64)
+        for a, b in ((0, HALF), (HALF, S)):
+            nc.vector.tensor_copy(x_codes[:, a:b], word_table[:].bitcast(U32).indirect(entries(offs_t, a, b)))
+
+        w2_raw = sb.tile([P, 4, 512], F32, name="w2_raw", tag="after_words", align_bytes=64)
         nc.sync.dma_start(w2_raw[:], w2.rearrange("(p j) c -> p j c", j=4))
 
-        neg_st = [sb.tile([P, S], F32, name=f"neg_st{t}") for t in range(4)]
+        plain = [sb.tile([P, S], F32, name=f"plain{t}") for t in range(4)]
+        def multiply_x(t, acc, a, b):
+            nc.tensor.matmul_mx(
+                out=acc[:, a:b], lhsT=w1_codes[t][:].bitcast(FP8X4), lhsT_scale=w1_planes[t][:],
+                rhs=x_codes[:, a:b].bitcast(FP8X4), rhs_scale=x_plane[:, a:b], start=True, stop=True,
+            )
+
+        for u, (a, b) in enumerate(((0, HALF), (HALF, S))):
+            y_half = psum.tile([P, S], F32, name=f"y_half{u}", tag=f"bank{u}")
+            multiply_x(0, y_half, a, b)
+            nc.scalar.activation(windows[0][:, a:b], y_half[:, a:b], COPY, scale=gain[:, 0:1])
+            nc.vector.tensor_copy(plain[0][:, a:b], windows[0][:, a:b])
+        for t in range(1, 4):
+            y_ps = psum.tile([P, S], F32, name=f"y_ps{t}", tag=f"bank{t + 1}")
+            multiply_x(t, y_ps, 0, S)
+            nc.scalar.activation(windows[t][:, :S], y_ps[:], COPY, scale=gain[:, t : t + 1])
+            nc.scalar.activation(plain[t][:], y_ps[:], COPY, scale=gain[:, t : t + 1])
+
+        neg_st = [sb.tile([P, S], F32, name=f"neg_st{t}", tag=f"after_st{t}", align_bytes=64) for t in range(4)]
         twice = [sb.tile([P, S], F32, name=f"twice{t}") for t in range(4)]
         for t in range(4):
-            nc.vector.tensor_tensor(neg_st[t][:], windows[t][:].indirect(n1_t[:]), plain[t][:], ALU.subtract)
+            for a, b in ((0, HALF), (HALF, S)) if t == 0 else ((0, S),):
+                nc.vector.tensor_tensor(neg_st[t][:, a:b], windows[t][:].indirect(entries(n1_t, a, b)), plain[t][:, a:b], ALU.subtract)
             nc.scalar.activation(twice[t][:], neg_st[t][:], COPY, scale=2.0)
 
-        z_bf = []
-        for u in range(2):
-            cols = slice(u * HALF, (u + 1) * HALF)
-            z4 = sb.tile([P, 4, HALF], F32, name=f"z4_{u}")
-            for t in range(4):
-                nc.vector.tensor_tensor(
-                    z4[:, t, :], neg_st[t][:].indirect(n1_t[:, u * 16 : (u + 1) * 16]), twice[t][:, cols], ALU.subtract
-                )
-            zb = sb.tile([P, HALF, 4], BF16, name=f"z_bf{u}", align_bytes=64)
-            nc.scalar.activation(
-                zb[:].rearrange("p (c i) t -> p c t i", i=4), z4[:].rearrange("p t (c i) -> p c t i", i=4), COPY, scale=0.5
-            )
-            z_bf.append(zb)
-
-        w2_codes = [sb.tile([P, P], U32, name=f"w2_codes{t}", align_bytes=64) for t in range(4)]
-        w2_planes = [sb.tile([P, P], U8, name=f"w2_plane{t}", align_bytes=64) for t in range(4)]
-        w2_bf = [sb.tile([P, P, 4], BF16, name=f"w2_bf{t}", align_bytes=64) for t in range(4)]
         w2_view = w2_raw[:].rearrange("p j (b t r) -> p t b r j", t=4, r=8)
-        z_codes = [sb.tile([P, HALF], U32, name=f"z_codes{u}", align_bytes=64) for u in range(2)]
-        z_planes = [sb.tile([P, HALF], U8, name=f"z_plane{u}", align_bytes=64) for u in range(2)]
+        w2_groups = ((0,), (1, 2), (3,))
+        w2_bf = []
+        w2_operand = {}
 
-        def quantize_z(u):
+        def cast_w2(u, tag):
+            w2_bf.append(sb.tile([P, len(w2_groups[u]), P, 4], BF16, name=f"w2_bf{u}", tag=tag, align_bytes=64))
+            for k, t in enumerate(w2_groups[u]):
+                nc.scalar.copy(w2_bf[u][:, k].rearrange("p (b r) j -> p b r j", r=8), w2_view[:, t])
+
+        def quantize_w2(u, tag):
+            width = len(w2_groups[u]) * P
+            codes = sb.tile([P, width], U32, name=f"w2_codes{u}", tag=tag, align_bytes=64)
+            plane = sb.tile([P, width], U8, name=f"w2_plane{u}", align_bytes=64)
+            nc.vector.quantize_mx(out=codes[:].bitcast(FP8X4), scales=plane[:], in_=w2_bf[u][:].rearrange("p t m j -> p (t m j)"))
+            for k, t in enumerate(w2_groups[u]):
+                w2_operand[t] = (codes[:, k * P : (k + 1) * P].bitcast(FP8X4), plane[:, k * P : (k + 1) * P])
+
+        cast_w2(0, "w2_bf0")
+        cast_w2(1, "w2_bf1")
+        z_bf, z_codes, z_planes = [], [], []
+        for i, (a, b) in enumerate(Z_SLICES):
+            z4 = sb.tile([P, 4, b - a], F32, name=f"z4_{i}")
+            for t in range(4):
+                nc.vector.tensor_tensor(z4[:, t, :], neg_st[t][:].indirect(entries(n1_t, a, b)), twice[t][:, a:b], ALU.subtract)
+            z_bf.append(sb.tile([P, b - a, 4], BF16, name=f"z_bf{i}", tag=f"after_z{i}", align_bytes=64))
+            nc.scalar.activation(
+                z_bf[i][:].rearrange("p (c i) t -> p c t i", i=4), z4[:].rearrange("p t (c i) -> p c t i", i=4), COPY, scale=0.5
+            )
+        quantize_w2(0, "after_st2")
+        for i, (a, b) in enumerate(Z_SLICES):
+            z_codes.append(sb.tile([P, b - a], U32, name=f"z_codes{i}", align_bytes=64))
+            z_planes.append(sb.tile([P, b - a], U8, name=f"z_plane{i}", align_bytes=64))
             nc.vector.quantize_mx(
-                out=z_codes[u][:].bitcast(FP8X4), scales=z_planes[u][:], in_=z_bf[u][:].rearrange("p c t -> p (c t)")
+                out=z_codes[i][:].bitcast(FP8X4), scales=z_planes[i][:], in_=z_bf[i][:].rearrange("p c t -> p (c t)")
+            )
+        quantize_w2(1, f"after_z{len(Z_SLICES) - 1}")
+
+        def multiply_z(t, i, acc):
+            a, b = Z_SLICES[i]
+            nc.tensor.matmul_mx(
+                out=acc[:, a:b], lhsT=w2_operand[t][0], lhsT_scale=w2_operand[t][1],
+                rhs=z_codes[i][:].bitcast(FP8X4), rhs_scale=z_planes[i][:], start=True, stop=True,
             )
 
-        def quantize_w2(t):
-            nc.vector.quantize_mx(
-                out=w2_codes[t][:].bitcast(FP8X4), scales=w2_planes[t][:], in_=w2_bf[t][:].rearrange("p m j -> p (m j)")
-            )
-
-        def cast_w2(t):
-            nc.vector.tensor_copy(w2_bf[t][:].rearrange("p (b r) j -> p b r j", r=8), w2_view[:, t])
-
-        quantize_z(0)
-        cast_w2(0)
-        cast_w2(1)
-        quantize_w2(0)
-        quantize_z(1)
-        quantize_w2(1)
-        cast_w2(2)
-        cast_w2(3)
-        quantize_w2(2)
-        quantize_w2(3)
-
-        for t in range(4):
-            for u in range(2):
-                nc.tensor.matmul_mx(
-                    out=h_ps[t][:, u * HALF : (u + 1) * HALF], lhsT=w2_codes[t][:].bitcast(FP8X4), lhsT_scale=w2_planes[t][:],
-                    rhs=z_codes[u][:].bitcast(FP8X4), rhs_scale=z_planes[u][:], start=True, stop=True,
-                )
-            nc.scalar.copy(windows[t][:, :S], h_ps[t][:])
-            nc.scalar.copy(plain[t][:], h_ps[t][:])
+        last = Z_SLICES[-1][0]
+        h_early = psum.tile([P, S], F32, name="h_early", tag="bank0")
+        h_late = psum.tile([P, S], F32, name="h_late", tag="bank1")
+        for i in range(len(Z_SLICES) - 1):
+            multiply_z(0, i, h_early)
+        multiply_z(0, len(Z_SLICES) - 1, h_late)
+        nc.scalar.copy(windows[0][:, :last], h_early[:, :last])
+        nc.vector.tensor_copy(plain[0][:, :last], windows[0][:, :last])
+        nc.scalar.copy(windows[0][:, last:S], h_late[:, last:])
+        nc.scalar.copy(plain[0][:, last:], h_late[:, last:])
+        for t in range(1, 4):
+            if t == 3:
+                cast_w2(2, f"after_z{len(Z_SLICES) - 1}")
+                quantize_w2(2, "w2_codes2")
+            h_ps = psum.tile([P, S], F32, name=f"h_ps{t}", tag=f"bank{t + 4}")
+            for i in range(len(Z_SLICES)):
+                multiply_z(t, i, h_ps)
+            nc.scalar.copy(windows[t][:, :S], h_ps[:])
+            nc.scalar.copy(plain[t][:], h_ps[:])
 
         out_view = out.rearrange("(b t r) n -> t b r n", t=4, r=8)
         pieces = [(0, 0, S), (1, 0, S), (2, 0, S), (3, 0, HALF), (3, HALF, S)]
-        held = {}
+        to_a, to_b, upper, offset = {}, {}, {}, {}
 
-        def fetch(i):
+        def fetch_a(i):
             t, a, b = pieces[i]
-            d1 = sb.tile([P, b - a], F32, name=f"d1_{i}")
-            d2 = sb.tile([P, b - a], F32, name=f"d2_{i}")
-            nc.vector.tensor_tensor(d1[:], windows[t][:].indirect(n2_t[:, a // 16 : b // 16]), plain[t][:, a:b], ALU.subtract)
-            nc.vector.tensor_tensor(d2[:], windows[t][:].indirect(n3_t[:, a // 16 : b // 16]), plain[t][:, a:b], ALU.subtract)
-            held[i] = (d1, d2)
+            to_a[i] = sb.tile([P, b - a], F32, name=f"to_a{i}")
+            for lo, hi in ((0, HALF), (HALF, S)) if i == 0 else ((a, b),):
+                nc.vector.tensor_tensor(to_a[i][:, lo - a : hi - a], windows[t][:].indirect(entries(n2_t, lo, hi)), plain[t][:, lo:hi], ALU.subtract)
 
-        def finish(i):
+        def fetch_b(i):
             t, a, b = pieces[i]
-            d1, d2 = held[i]
-            upper = sb.tile([P, b - a], F32, name=f"upper{i}")
-            mid = sb.tile([P, b - a], F32, name=f"mid{i}")
+            to_b[i] = sb.tile([P, b - a], F32, name=f"to_b{i}")
+            nc.vector.tensor_tensor(to_b[i][:], windows[t][:].indirect(entries(n3_t, a, b)), plain[t][:, a:b], ALU.subtract)
+
+        def clip_above(i):
+            t, a, b = pieces[i]
+            upper[i] = sb.tile([P, b - a], F32, name=f"upper{i}")
+            nc.vector.scalar_tensor_tensor(upper[i][:], to_a[i][:], 0.0, to_b[i][:], ALU.max, ALU.min)
+
+        def clip_below(i):
+            t, a, b = pieces[i]
+            offset[i] = sb.tile([P, b - a], F32, name=f"offset{i}")
+            nc.vector.scalar_tensor_tensor(offset[i][:], to_a[i][:], 0.0, upper[i][:], ALU.min, ALU.max)
+
+        def add_on_vector(i):
+            t, a, b = pieces[i]
             res = sb.tile([P, b - a], F32, name=f"res{i}")
-            nc.vector.scalar_tensor_tensor(upper[:], d1[:], 0.0, d2[:], ALU.max, ALU.min)
-            nc.vector.scalar_tensor_tensor(mid[:], d1[:], 0.0, upper[:], ALU.min, ALU.max)
-            nc.vector.tensor_tensor(res[:], mid[:], plain[t][:, a:b], ALU.add)
+            nc.vector.tensor_tensor(res[:], offset[i][:], plain[t][:, a:b], ALU.add)
             nc.sync.dma_start(out_view[t][:, :, a:b], res[:])
 
+        def add_on_tensor(i):
+            t, a, b = pieces[i]
+            res = sb.tile([P, b - a], F32, name=f"res{i}")
+            for lo in range(a, b, HALF):
+                u = lo // HALF
+                turned_ps = psum.tile([P, S], F32, name=f"turned_ps{t}_{u}", tag=f"bank{u}")
+                back_ps = psum.tile([P, S], F32, name=f"back_ps{t}_{u}", tag=f"bank{2 + u}")
+                turned = sb.tile([P, HALF], F32, name=f"turned{t}_{u}")
+                for c in range(0, HALF, P):
+                    nc.tensor.matmul(turned_ps[:, c : c + P], plain[t][:, lo + c : lo + c + P], ident[:], start=True, stop=False, is_transpose=True)
+                    nc.tensor.matmul(turned_ps[:, c : c + P], offset[i][:, lo - a + c : lo - a + c + P], ident[:], start=False, stop=True, is_transpose=True)
+                nc.scalar.copy(turned[:], turned_ps[:, :HALF])
+                for c in range(0, HALF, P):
+                    nc.tensor.transpose(back_ps[:, c : c + P], turned[:, c : c + P], ident[:])
+                nc.scalar.copy(res[:, lo - a : lo - a + HALF], back_ps[:, :HALF])
+            nc.sync.dma_start(out_view[t][:, :, a:b], res[:])
+
+        fetch_a(0)
+        fetch_b(0)
         for i in range(len(pieces)):
-            fetch(i)
-            finish(i)
+            more = i + 1 < len(pieces)
+            if more:
+                fetch_a(i + 1)
+            clip_above(i)
+            if more:
+                fetch_b(i + 1)
+            clip_below(i)
+            if pieces[i][0] < 3:
+                add_on_tensor(i)
+            else:
+                add_on_vector(i)

@@ -14,11 +14,16 @@ ALU = mybir.AluOpType
 COPY = mybir.ActivationFunctionType.Copy
 
 P = 128
-T, S = 2048, 512
+T = 2048
+S = 512
+QUARTERS = 4
+LAST = QUARTERS - 1
 HALF = S // 2
-LIST_COLS = S // 16
-FLOPS = 2 * 2 * 512 * 512 * 512
-Z_SLICES = ((0, 256), (256, 384), (384, 512))
+HALVES = ((0, HALF), (HALF, S))
+WHOLE = ((0, S),)
+GROUP = 16
+SCALAR_SHARE = 128
+FLOPS = 2 * 2 * S * S * S
 
 
 def tile_picked_hashtwicemed_none_p_kernel(
@@ -30,36 +35,54 @@ def tile_picked_hashtwicemed_none_p_kernel(
         sb = ctx.enter_context(tc.tile_pool(name="sb", bufs=1))
         psum = ctx.enter_context(tc.psum_pool(name="psum", bufs=1))
 
-        offs_t = lists.tile([P, LIST_COLS], U16, name="offs_t")
-        n1_t = lists.tile([P, LIST_COLS], U16, name="n1_t")
-        n2_t = lists.tile([P, LIST_COLS], U16, name="n2_t")
-        n3_t = lists.tile([P, LIST_COLS], U16, name="n3_t")
 
         def entries(list_tile, a, b):
-            return list_tile[:, a // 16 : b // 16]
+            return list_tile[:, a // GROUP : b // GROUP]
 
-        scale_table = sb.tile([P, T], U8, name="scale_table", tag="after_scales", align_bytes=64)
-        x_plane = sb.tile([P, S], U8, name="x_plane", align_bytes=64)
-        word_table = sb.tile([P, T], I32, name="word_table", tag="after_words", align_bytes=64)
-        w1_raw = sb.tile([P, 4, 512], F32, name="w1_raw")
-        gain = sb.tile([P, 4], F32, name="gain")
+        def quantize(name, grouped, width, tag):
+            codes = sb.tile([P, width], U32, name=f"{name}_codes", tag=tag, align_bytes=64)
+            scales = sb.tile([P, width], U8, name=f"{name}_scales", align_bytes=64)
+            nc.vector.quantize_mx(out=codes[:].bitcast(FP8X4), scales=scales[:], in_=grouped)
+            return codes, scales
+
+        def multiply(acc, weights, m, moving, cols):
+            m_cols = slice(m * P, (m + 1) * P)
+            nc.tensor.matmul_mx(
+                out=acc,
+                lhsT=weights[0][:, m_cols].bitcast(FP8X4),
+                lhsT_scale=weights[1][:, m_cols],
+                rhs=moving[0][:, cols].bitcast(FP8X4),
+                rhs_scale=moving[1][:, cols],
+                start=True,
+                stop=True,
+            )
+
+        offs_t = lists.tile([P, S // GROUP], U16, name="offs_t")
+        n1_t = lists.tile([P, S // GROUP], U16, name="n1_t")
+        n2_t = lists.tile([P, S // GROUP], U16, name="n2_t")
+        n3_t = lists.tile([P, S // GROUP], U16, name="n3_t")
+        scale_table = sb.tile([P, T], U8, name="scale_table", tag="after_scale_table", align_bytes=64)
+        x_scales_placed = sb.tile([P, S], U8, name="x_scales_placed", align_bytes=64)
+        word_table = sb.tile([P, T], I32, name="word_table", tag="after_word_table", align_bytes=64)
+        w1_raw = sb.tile([P, 4, S], F32, name="w1_raw")
+        gain = sb.tile([P, QUARTERS], F32, name="gain")
         ident = sb.tile([P, P], F32, name="ident")
 
-        scale_words = scale_table[:].bitcast(I32)
-        nc.vector.memset(scale_words[:, : T // 8], 0)
-        nc.gpsimd.memset(scale_words[:, T // 8 :], 0)
-        nc.vector.memset(x_plane[:].bitcast(I32), 0)
+        scale_table_words = scale_table[:].bitcast(I32)
+        nc.vector.memset(scale_table_words[:, : T // 8], 0)
+        nc.gpsimd.memset(scale_table_words[:, T // 8 :], 0)
+        nc.vector.memset(x_scales_placed[:].bitcast(I32), 0)
         nc.sync.dma_start(offs_t[:], offs)
-        nc.sync.dma_start(gain[:], gn.rearrange("(p t) o -> p (t o)", t=4))
+        nc.sync.dma_start(n1_t[:], n1)
         nc.sync.dma_start(scale_table[0:P:8, :].bitcast(I32), x_scales[0].bitcast(I32))
         nc.sync.dma_start(w1_raw[:], w1.rearrange("(p j) c -> p j c", j=4))
         nc.sync.dma_start(word_table[:], x_words[0].rearrange("p c r -> p (c r)").bitcast(I32))
-        nc.sync.dma_start(n1_t[:], n1)
+        nc.sync.dma_start(gain[:], gn.rearrange("(p t) o -> p (t o)", t=QUARTERS))
         nc.sync.dma_start(n2_t[:], n2)
         nc.sync.dma_start(n3_t[:], n3)
 
-        windows = [sb.tile([P, 2 * S], F32, name=f"window{t}") for t in range(4)]
-        for t in range(0, 4, 2):
+        windows = [sb.tile([P, 2 * S], F32, name=f"window{t}") for t in range(QUARTERS)]
+        for t in range(0, QUARTERS, 2):
             nc.vector.memset(windows[t][:, S:], 0.0)
             nc.scalar.copy(windows[t + 1][:, S:], windows[t][:, S:])
         make_identity(nc, ident[:])
@@ -67,179 +90,152 @@ def tile_picked_hashtwicemed_none_p_kernel(
         picked_scales = sb.tile([P, S], U8, name="picked_scales", align_bytes=64)
         nc.vector.tensor_copy(picked_scales[:], scale_table[:].indirect(offs_t[:]))
         for s in range(4):
-            nc.scalar.dma_start(x_plane[s:P:32, :].bitcast(I32), picked_scales[8 * s : P : 32, :].bitcast(I32))
+            nc.scalar.dma_start(x_scales_placed[s:P:32, :].bitcast(I32), picked_scales[8 * s : P : 32, :].bitcast(I32))
 
-        w1_codes = [sb.tile([P, P], U32, name=f"w1_codes{t}", align_bytes=64) for t in range(4)]
-        w1_planes = [sb.tile([P, P], U8, name=f"w1_plane{t}", align_bytes=64) for t in range(4)]
-        w1_lo = sb.tile([P, 2, P, 4], BF16, name="w1_lo", tag="after_scales", align_bytes=64)
+        w1_view = w1_raw[:].rearrange("p j (m t) -> p m t j", t=QUARTERS)
+        w1_lo = sb.tile([P, 2, P, 4], BF16, name="w1_lo", tag="after_scale_table", align_bytes=64)
         w1_hi = sb.tile([P, 2, P, 4], BF16, name="w1_hi", align_bytes=64)
-        w1_bf = [w1_lo, w1_hi]
-        w1_view = w1_raw[:].rearrange("p j (m t) -> p m t j", t=4)
         nc.vector.tensor_copy(w1_lo[:].rearrange("p t m j -> p m t j"), w1_view[:, :, 0:2, :])
         nc.scalar.copy(w1_hi[:].rearrange("p t m j -> p m t j"), w1_view[:, :, 2:4, :])
-        for t in range(4):
-            nc.vector.quantize_mx(
-                out=w1_codes[t][:].bitcast(FP8X4),
-                scales=w1_planes[t][:],
-                in_=w1_bf[t // 2][:, t % 2].rearrange("p m j -> p (m j)"),
-            )
+        w1_lo_mx = quantize("w1_lo", w1_lo[:].rearrange("p t m j -> p (t m j)"), 2 * P, "w1_lo_codes")
 
         x_codes = sb.tile([P, S], U32, name="x_codes", align_bytes=64)
-        for a, b in ((0, HALF), (HALF, S)):
+        for a, b in HALVES:
             nc.vector.tensor_copy(x_codes[:, a:b], word_table[:].bitcast(U32).indirect(entries(offs_t, a, b)))
+        x_mx = (x_codes, x_scales_placed)
+        w1_hi_mx = quantize("w1_hi", w1_hi[:].rearrange("p t m j -> p (t m j)"), 2 * P, "after_word_table")
+        w1_mx = (w1_lo_mx, w1_hi_mx)
 
-        w2_raw = sb.tile([P, 4, 512], F32, name="w2_raw", tag="after_words", align_bytes=64)
+        w2_raw = sb.tile([P, 4, S], F32, name="w2_raw", tag="after_word_table", align_bytes=64)
         nc.sync.dma_start(w2_raw[:], w2.rearrange("(p j) c -> p j c", j=4))
 
-        plain = [sb.tile([P, S], F32, name=f"plain{t}") for t in range(4)]
-        def multiply_x(t, acc, a, b):
-            nc.tensor.matmul_mx(
-                out=acc[:, a:b], lhsT=w1_codes[t][:].bitcast(FP8X4), lhsT_scale=w1_planes[t][:],
-                rhs=x_codes[:, a:b].bitcast(FP8X4), rhs_scale=x_plane[:, a:b], start=True, stop=True,
-            )
-
-        for u, (a, b) in enumerate(((0, HALF), (HALF, S))):
+        plain = [sb.tile([P, S], F32, name=f"plain{t}") for t in range(QUARTERS)]
+        for u, (a, b) in enumerate(HALVES):
             y_half = psum.tile([P, S], F32, name=f"y_half{u}", tag=f"bank{u}")
-            multiply_x(0, y_half, a, b)
+            multiply(y_half[:, a:b], w1_mx[0], 0, x_mx, slice(a, b))
             nc.scalar.activation(windows[0][:, a:b], y_half[:, a:b], COPY, scale=gain[:, 0:1])
             nc.vector.tensor_copy(plain[0][:, a:b], windows[0][:, a:b])
-        for t in range(1, 4):
+        for t in range(1, QUARTERS):
             y_ps = psum.tile([P, S], F32, name=f"y_ps{t}", tag=f"bank{t + 1}")
-            multiply_x(t, y_ps, 0, S)
+            multiply(y_ps[:], w1_mx[t // 2], t % 2, x_mx, slice(0, S))
             nc.scalar.activation(windows[t][:, :S], y_ps[:], COPY, scale=gain[:, t : t + 1])
             nc.scalar.activation(plain[t][:], y_ps[:], COPY, scale=gain[:, t : t + 1])
 
-        neg_st = [sb.tile([P, S], F32, name=f"neg_st{t}", tag=f"after_st{t}", align_bytes=64) for t in range(4)]
-        twice = [sb.tile([P, S], F32, name=f"twice{t}") for t in range(4)]
-        for t in range(4):
-            for a, b in ((0, HALF), (HALF, S)) if t == 0 else ((0, S),):
-                nc.vector.tensor_tensor(neg_st[t][:, a:b], windows[t][:].indirect(entries(n1_t, a, b)), plain[t][:, a:b], ALU.subtract)
+        neg_st = [sb.tile([P, S], F32, name=f"neg_st{t}", tag=f"after_neg_st{t}", align_bytes=64) for t in range(QUARTERS)]
+        twice = [sb.tile([P, S], F32, name=f"twice{t}") for t in range(QUARTERS)]
+        for t in range(QUARTERS):
+            for a, b in HALVES if t == 0 else WHOLE:
+                nc.vector.tensor_tensor(
+                    neg_st[t][:, a:b], windows[t][:].indirect(entries(n1_t, a, b)), plain[t][:, a:b], ALU.subtract
+                )
             nc.scalar.activation(twice[t][:], neg_st[t][:], COPY, scale=2.0)
 
-        w2_view = w2_raw[:].rearrange("p j (b t r) -> p t b r j", t=4, r=8)
-        w2_groups = ((0,), (1, 2), (3,))
-        w2_bf = []
-        w2_operand = {}
+        w2_view = w2_raw[:].rearrange("p j (b t c i) -> p t b c j i", t=QUARTERS, c=2, i=4)
 
-        def cast_w2(u, tag):
-            w2_bf.append(sb.tile([P, len(w2_groups[u]), P, 4], BF16, name=f"w2_bf{u}", tag=tag, align_bytes=64))
-            for k, t in enumerate(w2_groups[u]):
-                nc.scalar.copy(w2_bf[u][:, k].rearrange("p (b r) j -> p b r j", r=8), w2_view[:, t])
+        def round_w2(name, quarters, tag):
+            grouped = sb.tile([P, len(quarters), P, 4], BF16, name=name, tag=tag, align_bytes=64)
+            for k, t in enumerate(quarters):
+                nc.scalar.copy(grouped[:, k].rearrange("p (b c i) j -> p b c j i", c=2, i=4), w2_view[:, t])
+            return grouped[:].rearrange("p t m j -> p (t m j)")
 
-        def quantize_w2(u, tag):
-            width = len(w2_groups[u]) * P
-            codes = sb.tile([P, width], U32, name=f"w2_codes{u}", tag=tag, align_bytes=64)
-            plane = sb.tile([P, width], U8, name=f"w2_plane{u}", align_bytes=64)
-            nc.vector.quantize_mx(out=codes[:].bitcast(FP8X4), scales=plane[:], in_=w2_bf[u][:].rearrange("p t m j -> p (t m j)"))
-            for k, t in enumerate(w2_groups[u]):
-                w2_operand[t] = (codes[:, k * P : (k + 1) * P].bitcast(FP8X4), plane[:, k * P : (k + 1) * P])
+        w2_first = round_w2("w2_first", (0,), "w2_first")
+        w2_middle = round_w2("w2_middle", (1, 2), "w2_middle")
 
-        cast_w2(0, "w2_bf0")
-        cast_w2(1, "w2_bf1")
-        z_bf, z_codes, z_planes = [], [], []
-        for i, (a, b) in enumerate(Z_SLICES):
-            z4 = sb.tile([P, 4, b - a], F32, name=f"z4_{i}")
-            for t in range(4):
-                nc.vector.tensor_tensor(z4[:, t, :], neg_st[t][:].indirect(entries(n1_t, a, b)), twice[t][:, a:b], ALU.subtract)
-            z_bf.append(sb.tile([P, b - a, 4], BF16, name=f"z_bf{i}", tag=f"after_z{i}", align_bytes=64))
-            nc.scalar.activation(
-                z_bf[i][:].rearrange("p (c i) t -> p c t i", i=4), z4[:].rearrange("p t (c i) -> p c t i", i=4), COPY, scale=0.5
-            )
-        quantize_w2(0, "after_st2")
-        for i, (a, b) in enumerate(Z_SLICES):
-            z_codes.append(sb.tile([P, b - a], U32, name=f"z_codes{i}", align_bytes=64))
-            z_planes.append(sb.tile([P, b - a], U8, name=f"z_plane{i}", align_bytes=64))
-            nc.vector.quantize_mx(
-                out=z_codes[i][:].bitcast(FP8X4), scales=z_planes[i][:], in_=z_bf[i][:].rearrange("p c t -> p (c t)")
-            )
-        quantize_w2(1, f"after_z{len(Z_SLICES) - 1}")
+        def quarters_last(tile_ap):
+            return tile_ap.rearrange("p (c i) t -> p c t i", i=4)
 
-        def multiply_z(t, i, acc):
-            a, b = Z_SLICES[i]
-            nc.tensor.matmul_mx(
-                out=acc[:, a:b], lhsT=w2_operand[t][0], lhsT_scale=w2_operand[t][1],
-                rhs=z_codes[i][:].bitcast(FP8X4), rhs_scale=z_planes[i][:], start=True, stop=True,
-            )
+        def quarters_first(tile_ap):
+            return tile_ap.rearrange("p t (c i) -> p c t i", i=4)
 
-        last = Z_SLICES[-1][0]
-        h_early = psum.tile([P, S], F32, name="h_early", tag="bank0")
-        h_late = psum.tile([P, S], F32, name="h_late", tag="bank1")
-        for i in range(len(Z_SLICES) - 1):
-            multiply_z(0, i, h_early)
-        multiply_z(0, len(Z_SLICES) - 1, h_late)
-        nc.scalar.copy(windows[0][:, :last], h_early[:, :last])
-        nc.vector.tensor_copy(plain[0][:, :last], windows[0][:, :last])
-        nc.scalar.copy(windows[0][:, last:S], h_late[:, last:])
-        nc.scalar.copy(plain[0][:, last:], h_late[:, last:])
-        for t in range(1, 4):
-            if t == 3:
-                cast_w2(2, f"after_z{len(Z_SLICES) - 1}")
-                quantize_w2(2, "w2_codes2")
+        z_twice = [sb.tile([P, QUARTERS, HALF], F32, name=f"z_twice{u}") for u in range(2)]
+        z_bf = [sb.tile([P, HALF, QUARTERS], BF16, name=f"z_bf{u}", tag=f"after_z_bf{u}", align_bytes=64) for u in range(2)]
+        for u, (a, b) in enumerate(HALVES):
+            for t in range(QUARTERS):
+                nc.vector.tensor_tensor(
+                    z_twice[u][:, t, :], neg_st[t][:].indirect(entries(n1_t, a, b)), twice[t][:, a:b], ALU.subtract
+                )
+            cut = HALF if u == 0 else SCALAR_SHARE
+            nc.scalar.activation(quarters_last(z_bf[u][:, :cut]), quarters_first(z_twice[u][:, :, :cut]), COPY, scale=0.5)
+        w2_first_mx = quantize("w2_first", w2_first, P, "after_neg_st2")
+        nc.vector.tensor_scalar(
+            quarters_last(z_bf[1][:, SCALAR_SHARE:]), quarters_first(z_twice[1][:, :, SCALAR_SHARE:]), 0.5, None, ALU.mult
+        )
+        z_mx = [quantize(f"z{u}", z_bf[u][:].rearrange("p c t -> p (c t)"), HALF, f"z{u}_codes") for u in range(2)]
+        w2_middle_mx = quantize("w2_middle", w2_middle, 2 * P, "after_z_bf1")
+
+        h_halves = [psum.tile([P, S], F32, name=f"h_half{u}", tag=f"bank{u}") for u in range(2)]
+        for u, (a, b) in enumerate(HALVES):
+            multiply(h_halves[u][:, a:b], w2_first_mx, 0, z_mx[u], slice(0, HALF))
+        nc.scalar.copy(windows[0][:, :HALF], h_halves[0][:, :HALF])
+        nc.vector.tensor_copy(plain[0][:, :HALF], windows[0][:, :HALF])
+        nc.scalar.copy(windows[0][:, HALF:S], h_halves[1][:, HALF:])
+        nc.scalar.copy(plain[0][:, HALF:], h_halves[1][:, HALF:])
+
+        def make_h(t, weights, m):
             h_ps = psum.tile([P, S], F32, name=f"h_ps{t}", tag=f"bank{t + 4}")
-            for i in range(len(Z_SLICES)):
-                multiply_z(t, i, h_ps)
+            for u, (a, b) in enumerate(HALVES):
+                multiply(h_ps[:, a:b], weights, m, z_mx[u], slice(0, HALF))
             nc.scalar.copy(windows[t][:, :S], h_ps[:])
             nc.scalar.copy(plain[t][:], h_ps[:])
 
-        out_view = out.rearrange("(b t r) n -> t b r n", t=4, r=8)
-        pieces = [(0, 0, S), (1, 0, S), (2, 0, S), (3, 0, HALF), (3, HALF, S)]
-        to_a, to_b, upper, offset = {}, {}, {}, {}
+        make_h(1, w2_middle_mx, 0)
+        make_h(2, w2_middle_mx, 1)
+        w2_last = round_w2("w2_last", (LAST,), "after_z_bf1")
+        make_h(LAST, quantize("w2_last", w2_last, P, "w2_last_codes"), 0)
 
-        def fetch_a(i):
-            t, a, b = pieces[i]
-            to_a[i] = sb.tile([P, b - a], F32, name=f"to_a{i}")
-            for lo, hi in ((0, HALF), (HALF, S)) if i == 0 else ((a, b),):
-                nc.vector.tensor_tensor(to_a[i][:, lo - a : hi - a], windows[t][:].indirect(entries(n2_t, lo, hi)), plain[t][:, lo:hi], ALU.subtract)
+        out_view = out.rearrange("(b t r) n -> t b r n", t=QUARTERS, r=8)
+        to_a = [sb.tile([P, S], F32, name=f"to_a{t}") for t in range(QUARTERS)]
+        to_b = [sb.tile([P, S], F32, name=f"to_b{t}") for t in range(QUARTERS)]
+        upper = [sb.tile([P, S], F32, name=f"upper{t}") for t in range(QUARTERS)]
+        shift = [sb.tile([P, S], F32, name=f"shift{t}") for t in range(QUARTERS)]
+        result = [sb.tile([P, S], F32, name=f"result{t}") for t in range(QUARTERS)]
 
-        def fetch_b(i):
-            t, a, b = pieces[i]
-            to_b[i] = sb.tile([P, b - a], F32, name=f"to_b{i}")
-            nc.vector.tensor_tensor(to_b[i][:], windows[t][:].indirect(entries(n3_t, a, b)), plain[t][:, a:b], ALU.subtract)
+        def fetch(dst, list_tile, t, ranges):
+            for a, b in ranges:
+                nc.vector.tensor_tensor(
+                    dst[t][:, a:b], windows[t][:].indirect(entries(list_tile, a, b)), plain[t][:, a:b], ALU.subtract
+                )
 
-        def clip_above(i):
-            t, a, b = pieces[i]
-            upper[i] = sb.tile([P, b - a], F32, name=f"upper{i}")
-            nc.vector.scalar_tensor_tensor(upper[i][:], to_a[i][:], 0.0, to_b[i][:], ALU.max, ALU.min)
+        def clip_above(t, ranges):
+            for a, b in ranges:
+                nc.vector.scalar_tensor_tensor(upper[t][:, a:b], to_a[t][:, a:b], 0.0, to_b[t][:, a:b], ALU.max, ALU.min)
 
-        def clip_below(i):
-            t, a, b = pieces[i]
-            offset[i] = sb.tile([P, b - a], F32, name=f"offset{i}")
-            nc.vector.scalar_tensor_tensor(offset[i][:], to_a[i][:], 0.0, upper[i][:], ALU.min, ALU.max)
+        def clip_below(t, ranges):
+            for a, b in ranges:
+                nc.vector.scalar_tensor_tensor(shift[t][:, a:b], to_a[t][:, a:b], 0.0, upper[t][:, a:b], ALU.min, ALU.max)
 
-        def add_on_vector(i):
-            t, a, b = pieces[i]
-            res = sb.tile([P, b - a], F32, name=f"res{i}")
-            nc.vector.tensor_tensor(res[:], offset[i][:], plain[t][:, a:b], ALU.add)
-            nc.sync.dma_start(out_view[t][:, :, a:b], res[:])
-
-        def add_on_tensor(i):
-            t, a, b = pieces[i]
-            res = sb.tile([P, b - a], F32, name=f"res{i}")
-            for lo in range(a, b, HALF):
-                u = lo // HALF
+        def add_on_tensor(t):
+            for u, (a, b) in enumerate(HALVES):
                 turned_ps = psum.tile([P, S], F32, name=f"turned_ps{t}_{u}", tag=f"bank{u}")
                 back_ps = psum.tile([P, S], F32, name=f"back_ps{t}_{u}", tag=f"bank{2 + u}")
                 turned = sb.tile([P, HALF], F32, name=f"turned{t}_{u}")
                 for c in range(0, HALF, P):
-                    nc.tensor.matmul(turned_ps[:, c : c + P], plain[t][:, lo + c : lo + c + P], ident[:], start=True, stop=False, is_transpose=True)
-                    nc.tensor.matmul(turned_ps[:, c : c + P], offset[i][:, lo - a + c : lo - a + c + P], ident[:], start=False, stop=True, is_transpose=True)
+                    for term, first in ((plain[t], True), (shift[t], False)):
+                        nc.tensor.matmul(
+                            turned_ps[:, c : c + P], term[:, a + c : a + c + P], ident[:],
+                            start=first, stop=not first, is_transpose=True,
+                        )
                 nc.scalar.copy(turned[:], turned_ps[:, :HALF])
                 for c in range(0, HALF, P):
                     nc.tensor.transpose(back_ps[:, c : c + P], turned[:, c : c + P], ident[:])
-                nc.scalar.copy(res[:, lo - a : lo - a + HALF], back_ps[:, :HALF])
-            nc.sync.dma_start(out_view[t][:, :, a:b], res[:])
+                nc.scalar.copy(result[t][:, a:b], back_ps[:, :HALF])
+                nc.sync.dma_start(out_view[t][:, :, a:b], result[t][:, a:b])
 
-        fetch_a(0)
-        fetch_b(0)
-        for i in range(len(pieces)):
-            more = i + 1 < len(pieces)
-            if more:
-                fetch_a(i + 1)
-            clip_above(i)
-            if more:
-                fetch_b(i + 1)
-            clip_below(i)
-            if pieces[i][0] < 3:
-                add_on_tensor(i)
-            else:
-                add_on_vector(i)
+        fetch(to_a, n2_t, 0, HALVES)
+        fetch(to_b, n3_t, 0, WHOLE)
+        for t in range(LAST - 1):
+            fetch(to_a, n2_t, t + 1, WHOLE)
+            clip_above(t, WHOLE)
+            fetch(to_b, n3_t, t + 1, WHOLE)
+            clip_below(t, WHOLE)
+            add_on_tensor(t)
+        clip_above(LAST - 1, WHOLE)
+        fetch(to_a, n2_t, LAST, WHOLE)
+        clip_below(LAST - 1, WHOLE)
+        add_on_tensor(LAST - 1)
+        fetch(to_b, n3_t, LAST, HALVES)
+        clip_above(LAST, HALVES)
+        clip_below(LAST, HALVES)
+        for a, b in HALVES:
+            nc.vector.tensor_tensor(result[LAST][:, a:b], shift[LAST][:, a:b], plain[LAST][:, a:b], ALU.add)
+            nc.sync.dma_start(out_view[LAST][:, :, a:b], result[LAST][:, a:b])

@@ -33,14 +33,15 @@ def tile_picked_hashtwicemed_none_p_kernel(
     with ExitStack() as ctx:
         lists = ctx.enter_context(tc.tile_pool(name="lists", bufs=1))
         sb = ctx.enter_context(tc.tile_pool(name="sb", bufs=1))
+        after_z = ctx.enter_context(tc.tile_pool(name="after_z", bufs=1))
         psum = ctx.enter_context(tc.psum_pool(name="psum", bufs=1))
 
 
         def entries(list_tile, a, b):
             return list_tile[:, a // GROUP : b // GROUP]
 
-        def quantize(name, grouped, width, tag):
-            codes = sb.tile([P, width], U32, name=f"{name}_codes", tag=tag, align_bytes=64)
+        def quantize(name, grouped, width, codes_pool=sb, **place):
+            codes = codes_pool.tile([P, width], U32, name=f"{name}_codes", align_bytes=64, **place)
             scales = sb.tile([P, width], U8, name=f"{name}_scales", align_bytes=64)
             nc.vector.quantize_mx(out=codes[:].bitcast(FP8X4), scales=scales[:], in_=grouped)
             return codes, scales
@@ -97,13 +98,13 @@ def tile_picked_hashtwicemed_none_p_kernel(
         w1_hi = sb.tile([P, 2, P, 4], BF16, name="w1_hi", align_bytes=64)
         nc.vector.tensor_copy(w1_lo[:].rearrange("p t m j -> p m t j"), w1_view[:, :, 0:2, :])
         nc.scalar.copy(w1_hi[:].rearrange("p t m j -> p m t j"), w1_view[:, :, 2:4, :])
-        w1_lo_mx = quantize("w1_lo", w1_lo[:].rearrange("p t m j -> p (t m j)"), 2 * P, "w1_lo_codes")
+        w1_lo_mx = quantize("w1_lo", w1_lo[:].rearrange("p t m j -> p (t m j)"), 2 * P)
 
         x_codes = sb.tile([P, S], U32, name="x_codes", align_bytes=64)
         for a, b in HALVES:
             nc.vector.tensor_copy(x_codes[:, a:b], word_table[:].bitcast(U32).indirect(entries(offs_t, a, b)))
         x_mx = (x_codes, x_scales_placed)
-        w1_hi_mx = quantize("w1_hi", w1_hi[:].rearrange("p t m j -> p (t m j)"), 2 * P, "after_word_table")
+        w1_hi_mx = quantize("w1_hi", w1_hi[:].rearrange("p t m j -> p (t m j)"), 2 * P, tag="after_word_table")
         w1_mx = (w1_lo_mx, w1_hi_mx)
 
         w2_raw = sb.tile([P, 4, S], F32, name="w2_raw", tag="after_word_table", align_bytes=64)
@@ -114,7 +115,10 @@ def tile_picked_hashtwicemed_none_p_kernel(
             y_half = psum.tile([P, S], F32, name=f"y_half{u}", tag=f"bank{u}")
             multiply(y_half[:, a:b], w1_mx[0], 0, x_mx, slice(a, b))
             nc.scalar.activation(windows[0][:, a:b], y_half[:, a:b], COPY, scale=gain[:, 0:1])
-            nc.vector.tensor_copy(plain[0][:, a:b], windows[0][:, a:b])
+            if u == 0:
+                nc.vector.tensor_copy(plain[0][:, a:b], windows[0][:, a:b])
+            else:
+                nc.scalar.activation(plain[0][:, a:b], y_half[:, a:b], COPY, scale=gain[:, 0:1])
         for t in range(1, QUARTERS):
             y_ps = psum.tile([P, S], F32, name=f"y_ps{t}", tag=f"bank{t + 1}")
             multiply(y_ps[:], w1_mx[t // 2], t % 2, x_mx, slice(0, S))
@@ -132,14 +136,15 @@ def tile_picked_hashtwicemed_none_p_kernel(
 
         w2_view = w2_raw[:].rearrange("p j (b t c i) -> p t b c j i", t=QUARTERS, c=2, i=4)
 
-        def round_w2(name, quarters, tag):
-            grouped = sb.tile([P, len(quarters), P, 4], BF16, name=name, tag=tag, align_bytes=64)
+        def round_w2(name, quarters):
+            grouped = sb.tile([P, len(quarters), P, 4], BF16, name=name, align_bytes=64)
             for k, t in enumerate(quarters):
                 nc.scalar.copy(grouped[:, k].rearrange("p (b c i) j -> p b c j i", c=2, i=4), w2_view[:, t])
             return grouped[:].rearrange("p t m j -> p (t m j)")
 
-        w2_first = round_w2("w2_first", (0,), "w2_first")
-        w2_middle = round_w2("w2_middle", (1, 2), "w2_middle")
+        w2_first = round_w2("w2_first", (0,))
+        w2_middle = round_w2("w2_middle", (1, 2))
+        w2_last = round_w2("w2_last", (LAST,))
 
         def quarters_last(tile_ap):
             return tile_ap.rearrange("p (c i) t -> p c t i", i=4)
@@ -148,7 +153,10 @@ def tile_picked_hashtwicemed_none_p_kernel(
             return tile_ap.rearrange("p t (c i) -> p c t i", i=4)
 
         z_twice = [sb.tile([P, QUARTERS, HALF], F32, name=f"z_twice{u}") for u in range(2)]
-        z_bf = [sb.tile([P, HALF, QUARTERS], BF16, name=f"z_bf{u}", tag=f"after_z_bf{u}", align_bytes=64) for u in range(2)]
+        z_bf = [
+            sb.tile([P, HALF, QUARTERS], BF16, name="z_bf0", align_bytes=64),
+            after_z.tile([P, HALF, QUARTERS], BF16, name="z_bf1", offset=0, align_bytes=64),
+        ]
         for u, (a, b) in enumerate(HALVES):
             for t in range(QUARTERS):
                 nc.vector.tensor_tensor(
@@ -156,20 +164,19 @@ def tile_picked_hashtwicemed_none_p_kernel(
                 )
             cut = HALF if u == 0 else SCALAR_SHARE
             nc.scalar.activation(quarters_last(z_bf[u][:, :cut]), quarters_first(z_twice[u][:, :, :cut]), COPY, scale=0.5)
-        w2_first_mx = quantize("w2_first", w2_first, P, "after_neg_st2")
+        w2_first_mx = quantize("w2_first", w2_first, P, tag="after_neg_st2")
         nc.vector.tensor_scalar(
             quarters_last(z_bf[1][:, SCALAR_SHARE:]), quarters_first(z_twice[1][:, :, SCALAR_SHARE:]), 0.5, None, ALU.mult
         )
-        z_mx = [quantize(f"z{u}", z_bf[u][:].rearrange("p c t -> p (c t)"), HALF, f"z{u}_codes") for u in range(2)]
-        w2_middle_mx = quantize("w2_middle", w2_middle, 2 * P, "after_z_bf1")
+        z_mx = [quantize(f"z{u}", z_bf[u][:].rearrange("p c t -> p (c t)"), HALF) for u in range(2)]
+        w2_middle_mx = quantize("w2_middle", w2_middle, 2 * P, after_z, offset=0)
+        w2_last_mx = quantize("w2_last", w2_last, P, after_z, offset=4 * 2 * P)
 
         h_halves = [psum.tile([P, S], F32, name=f"h_half{u}", tag=f"bank{u}") for u in range(2)]
         for u, (a, b) in enumerate(HALVES):
             multiply(h_halves[u][:, a:b], w2_first_mx, 0, z_mx[u], slice(0, HALF))
-        nc.scalar.copy(windows[0][:, :HALF], h_halves[0][:, :HALF])
-        nc.vector.tensor_copy(plain[0][:, :HALF], windows[0][:, :HALF])
-        nc.scalar.copy(windows[0][:, HALF:S], h_halves[1][:, HALF:])
-        nc.scalar.copy(plain[0][:, HALF:], h_halves[1][:, HALF:])
+            nc.scalar.copy(windows[0][:, a:b], h_halves[u][:, a:b])
+            nc.scalar.copy(plain[0][:, a:b], h_halves[u][:, a:b])
 
         def make_h(t, weights, m):
             h_ps = psum.tile([P, S], F32, name=f"h_ps{t}", tag=f"bank{t + 4}")
@@ -180,8 +187,7 @@ def tile_picked_hashtwicemed_none_p_kernel(
 
         make_h(1, w2_middle_mx, 0)
         make_h(2, w2_middle_mx, 1)
-        w2_last = round_w2("w2_last", (LAST,), "after_z_bf1")
-        make_h(LAST, quantize("w2_last", w2_last, P, "w2_last_codes"), 0)
+        make_h(LAST, w2_last_mx, 0)
 
         out_view = out.rearrange("(b t r) n -> t b r n", t=QUARTERS, r=8)
         to_a = [sb.tile([P, S], F32, name=f"to_a{t}") for t in range(QUARTERS)]
@@ -205,20 +211,20 @@ def tile_picked_hashtwicemed_none_p_kernel(
                 nc.vector.scalar_tensor_tensor(shift[t][:, a:b], to_a[t][:, a:b], 0.0, upper[t][:, a:b], ALU.min, ALU.max)
 
         def add_on_tensor(t):
+            turned_ps = [psum.tile([P, S], F32, name=f"turned_ps{t}_{c}", tag=f"bank{c}") for c in range(S // P)]
+            turned = sb.tile([P, S], F32, name=f"turned{t}")
+            for term, first in ((plain[t], True), (shift[t], False)):
+                for c in range(S // P):
+                    nc.tensor.matmul(
+                        turned_ps[c][:, :P], term[:, c * P : (c + 1) * P], ident[:],
+                        start=first, stop=not first, is_transpose=True,
+                    )
             for u, (a, b) in enumerate(HALVES):
-                turned_ps = psum.tile([P, S], F32, name=f"turned_ps{t}_{u}", tag=f"bank{u}")
-                back_ps = psum.tile([P, S], F32, name=f"back_ps{t}_{u}", tag=f"bank{2 + u}")
-                turned = sb.tile([P, HALF], F32, name=f"turned{t}_{u}")
-                for c in range(0, HALF, P):
-                    for term, first in ((plain[t], True), (shift[t], False)):
-                        nc.tensor.matmul(
-                            turned_ps[:, c : c + P], term[:, a + c : a + c + P], ident[:],
-                            start=first, stop=not first, is_transpose=True,
-                        )
-                nc.scalar.copy(turned[:], turned_ps[:, :HALF])
-                for c in range(0, HALF, P):
-                    nc.tensor.transpose(back_ps[:, c : c + P], turned[:, c : c + P], ident[:])
-                nc.scalar.copy(result[t][:, a:b], back_ps[:, :HALF])
+                back_ps = psum.tile([P, S], F32, name=f"back_ps{t}_{u}", tag=f"bank{4 + u}")
+                for c in range(a // P, b // P):
+                    nc.scalar.copy(turned[:, c * P : (c + 1) * P], turned_ps[c][:, :P])
+                    nc.tensor.transpose(back_ps[:, c * P : (c + 1) * P], turned[:, c * P : (c + 1) * P], ident[:])
+                nc.scalar.copy(result[t][:, a:b], back_ps[:, a:b])
                 nc.sync.dma_start(out_view[t][:, :, a:b], result[t][:, a:b])
 
         fetch(to_a, n2_t, 0, HALVES)

from contextlib import ExitStack

import concourse.mybir as mybir
from concourse.masks import make_identity

F32 = mybir.dt.float32
BF16 = mybir.dt.bfloat16
I32 = mybir.dt.int32
U32 = mybir.dt.uint32
U16 = mybir.dt.uint16
U8 = mybir.dt.uint8
FP8X4 = mybir.dt.float8_e4m3fn_x4
ALU = mybir.AluOpType
COPY = mybir.ActivationFunctionType.Copy

P = 128
T = 2048
S = 512
QUARTERS = 4
LAST = QUARTERS - 1
HALF = S // 2
HALVES = ((0, HALF), (HALF, S))
WHOLE = ((0, S),)
GROUP = 16
SCALAR_SHARE = 128
FLOPS = 2 * 2 * S * S * S


def tile_picked_hashtwicemed_none_p_kernel(
    tc, x_words, x_scales, w1, gn, w2, offs, n1, n2, n3, out
):
    nc = tc.nc
    with ExitStack() as ctx:
        lists = ctx.enter_context(tc.tile_pool(name="lists", bufs=1))
        sb = ctx.enter_context(tc.tile_pool(name="sb", bufs=1))
        after_z = ctx.enter_context(tc.tile_pool(name="after_z", bufs=1))
        psum = ctx.enter_context(tc.psum_pool(name="psum", bufs=1))


        def entries(list_tile, a, b):
            return list_tile[:, a // GROUP : b // GROUP]

        def quantize(name, grouped, width, codes_pool=sb, **place):
            codes = codes_pool.tile([P, width], U32, name=f"{name}_codes", align_bytes=64, **place)
            scales = sb.tile([P, width], U8, name=f"{name}_scales", align_bytes=64)
            nc.vector.quantize_mx(out=codes[:].bitcast(FP8X4), scales=scales[:], in_=grouped)
            return codes, scales

        def multiply(acc, weights, m, moving, cols):
            m_cols = slice(m * P, (m + 1) * P)
            nc.tensor.matmul_mx(
                out=acc,
                lhsT=weights[0][:, m_cols].bitcast(FP8X4),
                lhsT_scale=weights[1][:, m_cols],
                rhs=moving[0][:, cols].bitcast(FP8X4),
                rhs_scale=moving[1][:, cols],
                start=True,
                stop=True,
            )

        offs_t = lists.tile([P, S // GROUP], U16, name="offs_t")
        n1_t = lists.tile([P, S // GROUP], U16, name="n1_t")
        n2_t = lists.tile([P, S // GROUP], U16, name="n2_t")
        n3_t = lists.tile([P, S // GROUP], U16, name="n3_t")
        scale_table = sb.tile([P, T], U8, name="scale_table", tag="after_scale_table", align_bytes=64)
        x_scales_placed = sb.tile([P, S], U8, name="x_scales_placed", align_bytes=64)
        word_table = sb.tile([P, T], I32, name="word_table", tag="after_word_table", align_bytes=64)
        w1_raw = sb.tile([P, 4, S], F32, name="w1_raw")
        gain = sb.tile([P, QUARTERS], F32, name="gain")
        ident = sb.tile([P, P], F32, name="ident")

        scale_table_words = scale_table[:].bitcast(I32)
        nc.vector.memset(scale_table_words[:, : T // 8], 0)
        nc.gpsimd.memset(scale_table_words[:, T // 8 :], 0)
        nc.vector.memset(x_scales_placed[:].bitcast(I32), 0)
        nc.sync.dma_start(offs_t[:], offs)
        nc.sync.dma_start(n1_t[:], n1)
        nc.sync.dma_start(scale_table[0:P:8, :].bitcast(I32), x_scales[0].bitcast(I32))
        nc.sync.dma_start(w1_raw[:], w1.rearrange("(p j) c -> p j c", j=4))
        nc.sync.dma_start(word_table[:], x_words[0].rearrange("p c r -> p (c r)").bitcast(I32))
        nc.sync.dma_start(gain[:], gn.rearrange("(p t) o -> p (t o)", t=QUARTERS))
        nc.sync.dma_start(n2_t[:], n2)
        nc.sync.dma_start(n3_t[:], n3)

        windows = [sb.tile([P, 2 * S], F32, name=f"window{t}") for t in range(QUARTERS)]
        for t in range(0, QUARTERS, 2):
            nc.vector.memset(windows[t][:, S:], 0.0)
            nc.scalar.copy(windows[t + 1][:, S:], windows[t][:, S:])
        make_identity(nc, ident[:])

        picked_scales = sb.tile([P, S], U8, name="picked_scales", align_bytes=64)
        nc.vector.tensor_copy(picked_scales[:], scale_table[:].indirect(offs_t[:]))
        for s in range(4):
            nc.scalar.dma_start(x_scales_placed[s:P:32, :].bitcast(I32), picked_scales[8 * s : P : 32, :].bitcast(I32))

        w1_view = w1_raw[:].rearrange("p j (m t) -> p m t j", t=QUARTERS)
        w1_lo = sb.tile([P, 2, P, 4], BF16, name="w1_lo", tag="after_scale_table", align_bytes=64)
        w1_hi = sb.tile([P, 2, P, 4], BF16, name="w1_hi", align_bytes=64)
        nc.vector.tensor_copy(w1_lo[:].rearrange("p t m j -> p m t j"), w1_view[:, :, 0:2, :])
        nc.scalar.copy(w1_hi[:].rearrange("p t m j -> p m t j"), w1_view[:, :, 2:4, :])
        w1_lo_mx = quantize("w1_lo", w1_lo[:].rearrange("p t m j -> p (t m j)"), 2 * P)

        x_codes = sb.tile([P, S], U32, name="x_codes", align_bytes=64)
        for a, b in HALVES:
            nc.vector.tensor_copy(x_codes[:, a:b], word_table[:].bitcast(U32).indirect(entries(offs_t, a, b)))
        x_mx = (x_codes, x_scales_placed)
        w1_hi_mx = quantize("w1_hi", w1_hi[:].rearrange("p t m j -> p (t m j)"), 2 * P, tag="after_word_table")
        w1_mx = (w1_lo_mx, w1_hi_mx)

        w2_raw = sb.tile([P, 4, S], F32, name="w2_raw", tag="after_word_table", align_bytes=64)
        nc.sync.dma_start(w2_raw[:], w2.rearrange("(p j) c -> p j c", j=4))

        plain = [sb.tile([P, S], F32, name=f"plain{t}") for t in range(QUARTERS)]
        for u, (a, b) in enumerate(HALVES):
            y_half = psum.tile([P, S], F32, name=f"y_half{u}", tag=f"bank{u}")
            multiply(y_half[:, a:b], w1_mx[0], 0, x_mx, slice(a, b))
            nc.scalar.activation(windows[0][:, a:b], y_half[:, a:b], COPY, scale=gain[:, 0:1])
            if u == 0:
                nc.vector.tensor_copy(plain[0][:, a:b], windows[0][:, a:b])
            else:
                nc.scalar.activation(plain[0][:, a:b], y_half[:, a:b], COPY, scale=gain[:, 0:1])
        for t in range(1, QUARTERS):
            y_ps = psum.tile([P, S], F32, name=f"y_ps{t}", tag=f"bank{t + 1}")
            multiply(y_ps[:], w1_mx[t // 2], t % 2, x_mx, slice(0, S))
            nc.scalar.activation(windows[t][:, :S], y_ps[:], COPY, scale=gain[:, t : t + 1])
            nc.scalar.activation(plain[t][:], y_ps[:], COPY, scale=gain[:, t : t + 1])

        neg_st = [sb.tile([P, S], F32, name=f"neg_st{t}", tag=f"after_neg_st{t}", align_bytes=64) for t in range(QUARTERS)]
        twice = [sb.tile([P, S], F32, name=f"twice{t}") for t in range(QUARTERS)]
        for t in range(QUARTERS):
            for a, b in HALVES if t == 0 else WHOLE:
                nc.vector.tensor_tensor(
                    neg_st[t][:, a:b], windows[t][:].indirect(entries(n1_t, a, b)), plain[t][:, a:b], ALU.subtract
                )
            nc.scalar.activation(twice[t][:], neg_st[t][:], COPY, scale=2.0)

        w2_view = w2_raw[:].rearrange("p j (b t c i) -> p t b c j i", t=QUARTERS, c=2, i=4)

        def round_w2(name, quarters):
            grouped = sb.tile([P, len(quarters), P, 4], BF16, name=name, align_bytes=64)
            for k, t in enumerate(quarters):
                nc.scalar.copy(grouped[:, k].rearrange("p (b c i) j -> p b c j i", c=2, i=4), w2_view[:, t])
            return grouped[:].rearrange("p t m j -> p (t m j)")

        w2_first = round_w2("w2_first", (0,))
        w2_middle = round_w2("w2_middle", (1, 2))
        w2_last = round_w2("w2_last", (LAST,))

        def quarters_last(tile_ap):
            return tile_ap.rearrange("p (c i) t -> p c t i", i=4)

        def quarters_first(tile_ap):
            return tile_ap.rearrange("p t (c i) -> p c t i", i=4)

        z_twice = [sb.tile([P, QUARTERS, HALF], F32, name=f"z_twice{u}") for u in range(2)]
        z_bf = [
            sb.tile([P, HALF, QUARTERS], BF16, name="z_bf0", align_bytes=64),
            after_z.tile([P, HALF, QUARTERS], BF16, name="z_bf1", offset=0, align_bytes=64),
        ]
        for u, (a, b) in enumerate(HALVES):
            for t in range(QUARTERS):
                nc.vector.tensor_tensor(
                    z_twice[u][:, t, :], neg_st[t][:].indirect(entries(n1_t, a, b)), twice[t][:, a:b], ALU.subtract
                )
            cut = HALF if u == 0 else SCALAR_SHARE
            nc.scalar.activation(quarters_last(z_bf[u][:, :cut]), quarters_first(z_twice[u][:, :, :cut]), COPY, scale=0.5)
        w2_first_mx = quantize("w2_first", w2_first, P, tag="after_neg_st2")
        nc.vector.tensor_scalar(
            quarters_last(z_bf[1][:, SCALAR_SHARE:]), quarters_first(z_twice[1][:, :, SCALAR_SHARE:]), 0.5, None, ALU.mult
        )
        z_mx = [quantize(f"z{u}", z_bf[u][:].rearrange("p c t -> p (c t)"), HALF) for u in range(2)]
        w2_middle_mx = quantize("w2_middle", w2_middle, 2 * P, after_z, offset=0)
        w2_last_mx = quantize("w2_last", w2_last, P, after_z, offset=4 * 2 * P)

        h_halves = [psum.tile([P, S], F32, name=f"h_half{u}", tag=f"bank{u}") for u in range(2)]
        for u, (a, b) in enumerate(HALVES):
            multiply(h_halves[u][:, a:b], w2_first_mx, 0, z_mx[u], slice(0, HALF))
            nc.scalar.copy(windows[0][:, a:b], h_halves[u][:, a:b])
            nc.scalar.copy(plain[0][:, a:b], h_halves[u][:, a:b])

        def make_h(t, weights, m):
            h_ps = psum.tile([P, S], F32, name=f"h_ps{t}", tag=f"bank{t + 4}")
            for u, (a, b) in enumerate(HALVES):
                multiply(h_ps[:, a:b], weights, m, z_mx[u], slice(0, HALF))
            nc.scalar.copy(windows[t][:, :S], h_ps[:])
            nc.scalar.copy(plain[t][:], h_ps[:])

        make_h(1, w2_middle_mx, 0)
        make_h(2, w2_middle_mx, 1)
        make_h(LAST, w2_last_mx, 0)

        out_view = out.rearrange("(b t r) n -> t b r n", t=QUARTERS, r=8)
        to_a = [sb.tile([P, S], F32, name=f"to_a{t}") for t in range(QUARTERS)]
        to_b = [sb.tile([P, S], F32, name=f"to_b{t}") for t in range(QUARTERS)]
        upper = [sb.tile([P, S], F32, name=f"upper{t}") for t in range(QUARTERS)]
        shift = [sb.tile([P, S], F32, name=f"shift{t}") for t in range(QUARTERS)]
        result = [sb.tile([P, S], F32, name=f"result{t}") for t in range(QUARTERS)]

        def fetch(dst, list_tile, t, ranges):
            for a, b in ranges:
                nc.vector.tensor_tensor(
                    dst[t][:, a:b], windows[t][:].indirect(entries(list_tile, a, b)), plain[t][:, a:b], ALU.subtract
                )

        def clip_above(t, ranges):
            for a, b in ranges:
                nc.vector.scalar_tensor_tensor(upper[t][:, a:b], to_a[t][:, a:b], 0.0, to_b[t][:, a:b], ALU.max, ALU.min)

        def clip_below(t, ranges):
            for a, b in ranges:
                nc.vector.scalar_tensor_tensor(shift[t][:, a:b], to_a[t][:, a:b], 0.0, upper[t][:, a:b], ALU.min, ALU.max)

        def add_on_tensor(t):
            turned_ps = [psum.tile([P, S], F32, name=f"turned_ps{t}_{c}", tag=f"bank{c}") for c in range(S // P)]
            turned = sb.tile([P, S], F32, name=f"turned{t}")
            for term, first in ((plain[t], True), (shift[t], False)):
                for c in range(S // P):
                    nc.tensor.matmul(
                        turned_ps[c][:, :P], term[:, c * P : (c + 1) * P], ident[:],
                        start=first, stop=not first, is_transpose=True,
                    )
            for u, (a, b) in enumerate(HALVES):
                back_ps = psum.tile([P, S], F32, name=f"back_ps{t}_{u}", tag=f"bank{4 + u}")
                for c in range(a // P, b // P):
                    nc.scalar.copy(turned[:, c * P : (c + 1) * P], turned_ps[c][:, :P])
                    nc.tensor.transpose(back_ps[:, c * P : (c + 1) * P], turned[:, c * P : (c + 1) * P], ident[:])
                nc.scalar.copy(result[t][:, a:b], back_ps[:, a:b])
                nc.sync.dma_start(out_view[t][:, :, a:b], result[t][:, a:b])

        fetch(to_a, n2_t, 0, HALVES)
        fetch(to_b, n3_t, 0, WHOLE)
        for t in range(LAST - 1):
            fetch(to_a, n2_t, t + 1, WHOLE)
            clip_above(t, WHOLE)
            fetch(to_b, n3_t, t + 1, WHOLE)
            clip_below(t, WHOLE)
            add_on_tensor(t)
        clip_above(LAST - 1, WHOLE)
        fetch(to_a, n2_t, LAST, WHOLE)
        clip_below(LAST - 1, WHOLE)
        add_on_tensor(LAST - 1)
        fetch(to_b, n3_t, LAST, HALVES)
        clip_above(LAST, HALVES)
        clip_below(LAST, HALVES)
        for a, b in HALVES:
            nc.vector.tensor_tensor(result[LAST][:, a:b], shift[LAST][:, a:b], plain[LAST][:, a:b], ALU.add)
            nc.sync.dma_start(out_view[LAST][:, :, a:b], result[LAST][:, a:b])
